import numpy as np
import ml_dtypes


def mxq(x, axis, fmt="e4m3"):
    dtype, down = {"e4m3": (ml_dtypes.float8_e4m3fn, 7), "e5m2": (ml_dtypes.float8_e5m2, 14)}[fmt]
    v = np.moveaxis(np.asarray(x, np.float32).astype(ml_dtypes.bfloat16).astype(np.float64), axis, -1)
    blocks = v.reshape(v.shape[:-1] + (-1, 32))
    amax = np.abs(blocks).max(-1, keepdims=True)
    byte = np.maximum(np.where(amax > 0, np.frexp(amax)[1] - 1 + 127, 0) - down, 1)
    scale = np.exp2(byte - 127.0)
    codes = (blocks / scale).astype(np.float32).astype(dtype).astype(np.float64)
    return np.moveaxis((codes * scale).reshape(v.shape), -1, axis)


WIDE = False


def mx_kscale(k):
    if not WIDE:
        return np.ones(k)
    levels = np.array([30, -30])
    if k % 512:
        return np.exp2(np.random.permutation(np.resize(levels, k // 32))).repeat(32)
    a = np.empty((k // 512, 16))
    for p in range(k // 512):
        a[p, :8] = np.random.permutation(np.resize(levels, 8))
        for g in range(8):
            far = levels[np.abs(levels - a[p, g]) >= 10]
            a[p, g + 8] = far[np.random.randint(len(far))]
    return np.exp2(a.ravel()).repeat(32)


def f64(x):
    return np.asarray(x).astype(np.float64)


def striped(idx):
    return np.tile(np.asarray(idx).reshape(-1, 16).T, (8, 1)).astype(np.uint16)


def unstriped(offs):
    return offs[:16].T.reshape(-1).astype(np.int64)


E2M1 = np.array([0.0, 0.5, 1.0, 1.5, 2.0, 3.0, 4.0, 6.0, -0.0, -0.5, -1.0, -1.5, -2.0, -3.0, -4.0, -6.0])


def pack_weight(w, fmt):
    k, n = w.shape
    w = f64(np.asarray(w, np.float32).astype(ml_dtypes.bfloat16)).reshape(k // 32, 32, n)
    amax = np.abs(w).max(1)
    if fmt in ("e4m3", "e5m2"):
        byte = np.frexp(amax)[1] - 1 + 127 - (7 if fmt == "e4m3" else 14)
    else:
        mant, ex = np.frexp(amax / 6.0)
        byte = np.where(mant > 0.5, ex, ex - 1) + 127
    byte = np.clip(np.where(amax > 0, byte, 1), 1, 254)
    scaled = (w * np.exp2(127.0 - byte)[:, None, :]).reshape(k, n).astype(np.float32)
    by_word = np.ascontiguousarray(scaled.reshape(k // 512, 128, 4, n).transpose(0, 1, 3, 2))
    if fmt in ("e4m3", "e5m2"):
        words = by_word.astype(ml_dtypes.float8_e4m3fn if fmt == "e4m3" else ml_dtypes.float8_e5m2).view(np.uint8)
    else:
        c = by_word.astype(ml_dtypes.float4_e2m1fn).view(np.uint8) & 0xF
        words = (c[..., 0::2] | (c[..., 1::2] << 4)).reshape(k // 512, 128, 2 * n)
    return np.ascontiguousarray(words), np.ascontiguousarray(byte.astype(np.uint8).reshape(k // 512, 16, n))


def unpack_weight(words, scales, fmt):
    g, _, n = scales.shape
    words = np.ascontiguousarray(words).reshape(g, 128, n, -1)
    if fmt in ("e4m3", "e5m2"):
        vals = words.view(ml_dtypes.float8_e4m3fn if fmt == "e4m3" else ml_dtypes.float8_e5m2).astype(np.float64)
    else:
        nib = np.empty((g, 128, n, 4), np.uint8)
        nib[..., 0::2] = words & 0xF
        nib[..., 1::2] = words >> 4
        vals = E2M1[nib]
    vals = vals * np.repeat(np.exp2(scales.astype(np.float64) - 127.0), 8, axis=1)[..., None]
    return vals.transpose(0, 1, 3, 2).reshape(g * 512, n)


def e4m3fn_bytes(y):
    return np.clip(np.asarray(y, np.float64), -448.0, 448.0).astype(np.float32).astype(ml_dtypes.float8_e4m3fn).view(np.uint8)


def e4m3fn_values(b):
    return np.asarray(b, np.uint8).view(ml_dtypes.float8_e4m3fn).astype(np.float64)


def sgn(shape):
    return np.random.uniform(0.5, 2.0, shape) * np.where(np.random.standard_normal(shape) < 0, -1.0, 1.0)


K, T, J, R, C, V, I, O, N = 512, 1024, 256, 512, 512, 512, 128, 256, 256


def setup_inputs():
    n = np.random.standard_normal
    idx = np.random.permutation(T)[:J]
    idx2 = np.random.permutation(J)[:I]
    idx3 = np.random.permutation(V)[:I]
    idx4 = np.random.permutation(C)[:I]
    idx5 = np.random.permutation(C)[:O]
    fk = mx_kscale(K)
    fr = mx_kscale(R)
    xtp = pack_weight(n((K, T)) / fk[:, None], "e5m2")
    wp = pack_weight(n((K, R)) * 1 / np.sqrt(K) * fk[:, None], "e2m1")
    wbp = pack_weight(n((R, N)) * 1 / np.sqrt(R) / fr[:, None], "e2m1")
    return {
        "xt_words": xtp[0],
        "xt_scales": xtp[1],
        "w_words": wp[0],
        "w_scales": wp[1],
        "ca": e4m3fn_bytes(60.0 * n((R, V))),
        "st": (np.random.uniform(0.004, 0.012, (R, 1)) * fr[:, None]).astype(np.float32),
        "sa": (sgn((R, 1))).astype(np.float32),
        "wb_words": wbp[0],
        "wb_scales": wbp[1],
        "offs": striped(idx),
        "offs2": striped(idx2),
        "offs3": striped(idx3),
        "offs4": striped(idx4),
        "offs5": striped(idx5),
    }


def reference(xt_words, xt_scales, w_words, w_scales, ca, st, sa, wb_words, wb_scales, offs, offs2, offs3, offs4, offs5):
    idx = unstriped(offs)
    idx2 = unstriped(offs2)
    idx3 = unstriped(offs3)
    idx4 = unstriped(offs4)
    idx5 = unstriped(offs5)
    xtu = unpack_weight(xt_words, xt_scales, "e5m2")
    wu = unpack_weight(w_words, w_scales, "e2m1")
    wbu = unpack_weight(wb_words, wb_scales, "e2m1")
    xtidxg = xtu[:, idx]
    a = wu.T @ xtidxg
    g1 = e4m3fn_values(ca)[:, idx3] * f64(st)
    h1 = a[:, idx2] * g1
    pw = np.zeros((R, C))
    pw[:, idx4] = h1 * f64(sa)
    hid = pw[:, idx5]
    hidq = mxq(hid, 0, "e4m3")
    p = wbu.T @ hidq
    return p

@@ -1,0 +1,163 @@
+from contextlib import ExitStack
+
+import concourse.mybir as mybir
+
+K, T, J, R, C, V, I, O, N = 512, 1024, 256, 512, 512, 512, 128, 256, 256
+FLOPS = 2 * K * R * J + 2 * R * N * O
+
+F32 = mybir.dt.float32
+BF16 = mybir.dt.bfloat16
+I32 = mybir.dt.int32
+U32 = mybir.dt.uint32
+U16 = mybir.dt.uint16
+U8 = mybir.dt.uint8
+E4M3 = mybir.dt.float8_e4m3fn
+E4M3X4 = mybir.dt.float8_e4m3fn_x4
+E5M2X4 = mybir.dt.float8_e5m2_x4
+E2M1X4 = mybir.dt.float4_e2m1fn_x4
+COPY = mybir.ActivationFunctionType.Copy
+MULT = mybir.AluOpType.mult
+
+P = 128
+PACK = 4
+HALF = O // 2
+
+
+def tile_list_relayed_kernel(tc, xt_words, xt_scales, w_words, w_scales, ca, st, sa, wb_words, wb_scales,
+                                offs, offs2, offs3, offs4, offs5, out):
+    nc = tc.nc
+    with ExitStack() as ctx:
+        sb = ctx.enter_context(tc.tile_pool(name="sb", bufs=1))
+        ps = ctx.enter_context(tc.psum_pool(name="ps", bufs=1))
+
+        l1 = sb.tile([P, J // 16], U16, name="l1")
+        l2 = sb.tile([P, I // 16], U16, name="l2")
+        l3 = sb.tile([P, I // 16], U16, name="l3")
+        l4 = sb.tile([P, I // 16], U16, name="l4")
+        l5 = sb.tile([P, O // 16], U16, name="l5")
+
+        xw = sb.tile([P, T], I32, name="xw", align_bytes=64)
+        xs = sb.tile([P, T], U8, name="xs", align_bytes=64)
+        xwg = sb.tile([P, J], U32, name="xwg", align_bytes=64)
+        xsg = sb.tile([P, J], U8, name="xsg", align_bytes=64)
+        ww = sb.tile([P, 2 * R], U8, name="ww", align_bytes=64)
+        wstage = sb.tile([PACK, R], I32, name="wstage", align_bytes=64)
+        wsraw = sb.tile([P, R], U8, name="wsraw", align_bytes=64)
+        wbw = sb.tile([P, 2 * N], U8, name="wbw", align_bytes=64)
+        wbs = sb.tile([P, N], U8, name="wbs", align_bytes=64)
+        st_t = sb.tile([P, PACK], F32, name="st_t")
+        sa_t = sb.tile([P, PACK], F32, name="sa_t")
+        cat = [sb.tile([P, V], U8, name=f"cat{t}", align_bytes=64) for t in range(PACK)]
+        pw = [sb.tile([P, C], F32, name=f"pw{t}", align_bytes=64) for t in range(PACK)]
+
+        nc.vector.memset(xs[:].bitcast(I32), 0)
+        nc.vector.memset(wsraw[:].bitcast(I32), 0)
+        nc.vector.memset(wbs[:].bitcast(I32), 0)
+        for t in range(PACK):
+            nc.vector.memset(pw[t][:], 0.0)
+
+        ca_rows = ca.rearrange("(p t) v -> t p v", t=PACK)
+        nc.sync.dma_start(l1[:], offs)
+        nc.scalar.dma_start(wstage[:].rearrange("r (q c) -> r q c", q=4),
+                            w_scales[0].bitcast(I32).rearrange("(q r) c -> r q c", r=4))
+        nc.sync.dma_start(xw[:], xt_words[0].rearrange("p c r -> p (c r)").bitcast(I32))
+        nc.sync.dma_start(ww[:].bitcast(I32), w_words[0].bitcast(I32))
+        for q in range(4):
+            nc.scalar.dma_start(xs[32 * q : 32 * q + 4, :].bitcast(I32), xt_scales[0, 4 * q : 4 * q + 4, :].bitcast(I32))
+        nc.gpsimd.dma_start(st_t[:], st.rearrange("(p t) o -> p (t o)", t=PACK))
+        nc.gpsimd.dma_start(sa_t[:], sa.rearrange("(p t) o -> p (t o)", t=PACK))
+        nc.sync.dma_start(l3[:], offs3)
+        nc.sync.dma_start(cat[0][:], ca_rows[0])
+        nc.sync.dma_start(l2[:], offs2)
+        nc.sync.dma_start(l4[:], offs4)
+        nc.sync.dma_start(cat[1][:], ca_rows[1])
+        nc.sync.dma_start(l5[:], offs5)
+        nc.sync.dma_start(cat[2][:], ca_rows[2])
+        nc.sync.dma_start(cat[3][:], ca_rows[3])
+        nc.sync.dma_start(wbw[:].bitcast(I32), wb_words[0].bitcast(I32))
+        for q in range(4):
+            nc.sync.dma_start(wbs[32 * q : 32 * q + 4, :].bitcast(I32), wb_scales[0, 4 * q : 4 * q + 4, :].bitcast(I32))
+
+        for q in range(4):
+            nc.vector.tensor_copy(wsraw[32 * q : 32 * q + 4, :].bitcast(I32), wstage[:, q * (R // 4) : (q + 1) * (R // 4)])
+        nc.vector.tensor_copy(xsg[:], xs[:].indirect(l1[:]))
+        wsd = [sb.tile([P, P], U8, name=f"wsd{t}", align_bytes=64) for t in range(PACK)]
+        wwd = [sb.tile([P, P], U16, name=f"wwd{t}", align_bytes=64) for t in range(PACK)]
+        ws_by_t = wsraw[:].rearrange("p (m t) -> p t m", t=PACK)
+        ww_by_t = ww[:].bitcast(U16).rearrange("p (m t) -> p t m", t=PACK)
+        nc.vector.tensor_copy(wsd[0][:], ws_by_t[:, 0, :])
+        nc.vector.tensor_copy(xwg[:], xw[:].bitcast(U32).indirect(l1[:]))
+        for t in range(PACK):
+            nc.scalar.copy(wwd[t][:], ww_by_t[:, t, :])
+
+        acc = [ps.tile([P, J], F32, name=f"acc{t}") for t in range(PACK)]
+        a_t = [sb.tile([P, J], F32, name=f"a{t}", align_bytes=64) for t in range(PACK)]
+        cg = [sb.tile([P, I], U8, name=f"cg{t}", align_bytes=64) for t in range(PACK)]
+        g1 = [sb.tile([P, I], F32, name=f"g{t}", align_bytes=64) for t in range(PACK)]
+        h1 = [sb.tile([P, I], F32, name=f"h{t}", tag=f"h{t}", align_bytes=64) for t in range(PACK)]
+        hid = [sb.tile([P, PACK * HALF], BF16, name="hid0", align_bytes=64)]
+
+        def first_product(t):
+            if t > 0:
+                nc.vector.tensor_copy(wsd[t][:], ws_by_t[:, t, :])
+            nc.tensor.matmul_mx(out=acc[t][:], lhsT=wwd[t][:].bitcast(E2M1X4), lhsT_scale=wsd[t][:],
+                                rhs=xwg[:].bitcast(E5M2X4), rhs_scale=xsg[:], start=True, stop=True)
+
+        def gates(t):
+            nc.vector.tensor_copy(cg[t][:], cat[t][:].indirect(l3[:]))
+            nc.vector.tensor_scalar(g1[t][:], cg[t][:].bitcast(E4M3), st_t[:, t : t + 1], None, MULT)
+
+        def seats(t):
+            if t < 2:
+                nc.scalar.copy(a_t[t][:], acc[t][:])
+            else:
+                nc.vector.tensor_copy(a_t[t][:], acc[t][:])
+            nc.vector.tensor_tensor(h1[t][:], a_t[t][:].indirect(l2[:]), g1[t][:], MULT)
+
+        def put(t):
+            nc.scalar.activation(pw[t][:].indirect(l4[:]), h1[t][:], COPY, scale=sa_t[:, t : t + 1])
+
+        def take(t, u):
+            cols = HALF // 16
+            nc.scalar.activation(hid[u][:].rearrange("p (c r) -> p c r", r=PACK)[:, :, t],
+                                 pw[t][:].indirect(l5[:, u * cols : (u + 1) * cols]), COPY)
+
+        def second_product(u):
+            hq = sb.tile([P, HALF], U32, name=f"hq{u}", align_bytes=64)
+            hs = sb.tile([P, HALF], U8, name=f"hs{u}", align_bytes=64)
+            nc.vector.quantize_mx(out=hq[:].bitcast(E4M3X4), scales=hs[:], in_=hid[u][:])
+            for h in range(2):
+                res = ps.tile([P, HALF], F32, name=f"res{u}{h}")
+                nc.tensor.matmul_mx(out=res[:], lhsT=wbw[:, 2 * P * h : 2 * P * (h + 1)].bitcast(E2M1X4),
+                                    lhsT_scale=wbs[:, P * h : P * (h + 1)],
+                                    rhs=hq[:].bitcast(E4M3X4), rhs_scale=hs[:], start=True, stop=True)
+                ot = sb.tile([P, HALF], F32, name=f"ot{u}{h}", align_bytes=64)
+                dst = out[P * h : P * (h + 1), HALF * u : HALF * (u + 1)]
+                if u == 1 and h == 1:
+                    nc.scalar.copy(ot[:], res[:])
+                    nc.scalar.dma_start(dst, ot[:])
+                else:
+                    nc.vector.tensor_copy(ot[:], res[:])
+                    nc.sync.dma_start(dst, ot[:])
+
+        first_product(0)
+        gates(0)
+        first_product(1)
+        seats(0)
+        gates(1)
+        seats(1)
+        put(0)
+        put(1)
+        for t in range(2, PACK):
+            first_product(t)
+            gates(t)
+            seats(t)
+            take(t - 2, 0)
+            put(t)
+        take(2, 0)
+        take(3, 0)
+        second_product(0)
+        hid.append(sb.tile([P, PACK * HALF], BF16, name="hid1", tag=f"h{PACK - 1}", align_bytes=64))
+        for t in range(PACK):
+            take(t, 1)
+        second_product(1)

@@ -37,8 +37,7 @@ def tile_list_relayed_kernel(tc, xt_words, xt_scales, w_words, w_scales, ca, st,
         l5 = sb.tile([P, O // 16], U16, name="l5")
 
         xw = sb.tile([P, T], I32, name="xw", align_bytes=64)
-        xs = sb.tile([P, T], U8, name="xs", align_bytes=64)
-        xwg = sb.tile([P, J], U32, name="xwg", align_bytes=64)
+        xs = sb.tile([P, T], U8, name="xs", tag="xs", align_bytes=64)
         xsg = sb.tile([P, J], U8, name="xsg", align_bytes=64)
         ww = sb.tile([P, 2 * R], U8, name="ww", align_bytes=64)
         wstage = sb.tile([PACK, R], I32, name="wstage", align_bytes=64)
@@ -52,28 +51,31 @@ def tile_list_relayed_kernel(tc, xt_words, xt_scales, w_words, w_scales, ca, st,
 
         nc.vector.memset(xs[:].bitcast(I32), 0)
         nc.vector.memset(wsraw[:].bitcast(I32), 0)
-        nc.vector.memset(wbs[:].bitcast(I32), 0)
+        nc.gpsimd.memset(wbs[:].bitcast(I32), 0)
         for t in range(PACK):
-            nc.vector.memset(pw[t][:], 0.0)
+            (nc.vector if t < 2 else nc.gpsimd).memset(pw[t][:], 0.0)
 
         ca_rows = ca.rearrange("(p t) v -> t p v", t=PACK)
+        def load_xs(queue, q):
+            queue.dma_start(xs[32 * q : 32 * q + 4, :].bitcast(I32), xt_scales[0, 4 * q : 4 * q + 4, :].bitcast(I32))
+
         nc.sync.dma_start(l1[:], offs)
         nc.scalar.dma_start(wstage[:].rearrange("r (q c) -> r q c", q=4),
                             w_scales[0].bitcast(I32).rearrange("(q r) c -> r q c", r=4))
-        nc.sync.dma_start(xw[:], xt_words[0].rearrange("p c r -> p (c r)").bitcast(I32))
-        nc.sync.dma_start(ww[:].bitcast(I32), w_words[0].bitcast(I32))
         for q in range(4):
-            nc.scalar.dma_start(xs[32 * q : 32 * q + 4, :].bitcast(I32), xt_scales[0, 4 * q : 4 * q + 4, :].bitcast(I32))
-        nc.gpsimd.dma_start(st_t[:], st.rearrange("(p t) o -> p (t o)", t=PACK))
-        nc.gpsimd.dma_start(sa_t[:], sa.rearrange("(p t) o -> p (t o)", t=PACK))
+            load_xs(nc.sync if q % 2 == 0 else nc.scalar, q)
+        nc.sync.dma_start(xw[:], xt_words[0].rearrange("p c r -> p (c r)").bitcast(I32))
+        nc.scalar.dma_start(ww[:].bitcast(I32), w_words[0].bitcast(I32))
         nc.sync.dma_start(l3[:], offs3)
+        nc.scalar.dma_start(st_t[:], st.rearrange("(p t) o -> p (t o)", t=PACK))
         nc.sync.dma_start(cat[0][:], ca_rows[0])
         nc.sync.dma_start(l2[:], offs2)
-        nc.sync.dma_start(l4[:], offs4)
         nc.sync.dma_start(cat[1][:], ca_rows[1])
-        nc.sync.dma_start(l5[:], offs5)
         nc.sync.dma_start(cat[2][:], ca_rows[2])
+        nc.sync.dma_start(sa_t[:], sa.rearrange("(p t) o -> p (t o)", t=PACK))
+        nc.sync.dma_start(l4[:], offs4)
         nc.sync.dma_start(cat[3][:], ca_rows[3])
+        nc.sync.dma_start(l5[:], offs5)
         nc.sync.dma_start(wbw[:].bitcast(I32), wb_words[0].bitcast(I32))
         for q in range(4):
             nc.sync.dma_start(wbs[32 * q : 32 * q + 4, :].bitcast(I32), wb_scales[0, 4 * q : 4 * q + 4, :].bitcast(I32))
@@ -81,37 +83,47 @@ def tile_list_relayed_kernel(tc, xt_words, xt_scales, w_words, w_scales, ca, st,
         for q in range(4):
             nc.vector.tensor_copy(wsraw[32 * q : 32 * q + 4, :].bitcast(I32), wstage[:, q * (R // 4) : (q + 1) * (R // 4)])
         nc.vector.tensor_copy(xsg[:], xs[:].indirect(l1[:]))
-        wsd = [sb.tile([P, P], U8, name=f"wsd{t}", align_bytes=64) for t in range(PACK)]
-        wwd = [sb.tile([P, P], U16, name=f"wwd{t}", align_bytes=64) for t in range(PACK)]
-        ws_by_t = wsraw[:].rearrange("p (m t) -> p t m", t=PACK)
+        wsd = sb.tile([P, PACK, P], U8, name="wsd", align_bytes=64)
+        wwd0 = sb.tile([P, P], U16, name="wwd0", align_bytes=64)
+        wwd1 = sb.tile([P, P], U16, name="wwd1", align_bytes=64)
+        wwdr = sb.tile([P, PACK - 2, P], U16, name="wwdr", align_bytes=64)
+        wwd = [wwd0[:], wwd1[:]] + [wwdr[:, t, :] for t in range(PACK - 2)]
         ww_by_t = ww[:].bitcast(U16).rearrange("p (m t) -> p t m", t=PACK)
-        nc.vector.tensor_copy(wsd[0][:], ws_by_t[:, 0, :])
-        nc.vector.tensor_copy(xwg[:], xw[:].bitcast(U32).indirect(l1[:]))
-        for t in range(PACK):
-            nc.scalar.copy(wwd[t][:], ww_by_t[:, t, :])
+        nc.vector.tensor_copy(wsd[:], wsraw[:].rearrange("p (m t) -> p t m", t=PACK))
+        xwg = sb.tile([P, J], U32, name="xwg", align_bytes=64)
+        for u in range(2):
+            nc.vector.tensor_copy(xwg[:, P * u : P * (u + 1)], xw[:].bitcast(U32).indirect(l1[:, 8 * u : 8 * (u + 1)]))
+        nc.scalar.copy(wwd0[:], ww_by_t[:, 0, :])
+        nc.scalar.copy(wwd1[:], ww_by_t[:, 1, :])
+        nc.scalar.copy(wwdr[:], ww_by_t[:, 2:, :])
 
-        acc = [ps.tile([P, J], F32, name=f"acc{t}") for t in range(PACK)]
-        a_t = [sb.tile([P, J], F32, name=f"a{t}", align_bytes=64) for t in range(PACK)]
-        cg = [sb.tile([P, I], U8, name=f"cg{t}", align_bytes=64) for t in range(PACK)]
-        g1 = [sb.tile([P, I], F32, name=f"g{t}", align_bytes=64) for t in range(PACK)]
-        h1 = [sb.tile([P, I], F32, name=f"h{t}", tag=f"h{t}", align_bytes=64) for t in range(PACK)]
-        hid = [sb.tile([P, PACK * HALF], BF16, name="hid0", align_bytes=64)]
+        acc01 = ps.tile([P, 2, J], F32, name="acc01")
+        acc2 = ps.tile([P, J], F32, name="acc2")
+        acc3 = ps.tile([P, J], F32, name="acc3")
+        acc = [acc01[:, 0, :], acc01[:, 1, :], acc2[:], acc3[:]]
+        a_t = [sb.tile([P, J], F32, name=f"a{t}", tag=f"a{t}", align_bytes=64) for t in range(2)]
+        cg = [sb.tile([P, I], U8, name=f"cg{t}", align_bytes=64) for t in range(PACK - 1)]
+        g1 = [sb.tile([P, I], F32, name=f"g{t}", tag=f"g{t}", align_bytes=64) for t in range(2)]
+        hid = []
+        h1 = []
 
-        def first_product(t):
-            if t > 0:
-                nc.vector.tensor_copy(wsd[t][:], ws_by_t[:, t, :])
-            nc.tensor.matmul_mx(out=acc[t][:], lhsT=wwd[t][:].bitcast(E2M1X4), lhsT_scale=wsd[t][:],
-                                rhs=xwg[:].bitcast(E5M2X4), rhs_scale=xsg[:], start=True, stop=True)
+        def first_product(t, cols):
+            nc.tensor.matmul_mx(out=acc[t][:, cols], lhsT=wwd[t].bitcast(E2M1X4), lhsT_scale=wsd[:, t, :],
+                                rhs=xwg[:, cols].bitcast(E5M2X4), rhs_scale=xsg[:, cols], start=True, stop=True)
+
+        def look_up(t):
+            nc.vector.tensor_copy(cg[t][:], cat[t][:].indirect(l3[:]))
 
         def gates(t):
-            nc.vector.tensor_copy(cg[t][:], cat[t][:].indirect(l3[:]))
             nc.vector.tensor_scalar(g1[t][:], cg[t][:].bitcast(E4M3), st_t[:, t : t + 1], None, MULT)
 
-        def seats(t):
+        def empty(t):
             if t < 2:
-                nc.scalar.copy(a_t[t][:], acc[t][:])
+                nc.scalar.copy(a_t[t][:], acc[t])
             else:
-                nc.vector.tensor_copy(a_t[t][:], acc[t][:])
+                nc.vector.tensor_copy(a_t[t][:], acc[t])
+
+        def seats(t):
             nc.vector.tensor_tensor(h1[t][:], a_t[t][:].indirect(l2[:]), g1[t][:], MULT)
 
         def put(t):
@@ -140,24 +152,40 @@ def tile_list_relayed_kernel(tc, xt_words, xt_scales, w_words, w_scales, ca, st,
                     nc.vector.tensor_copy(ot[:], res[:])
                     nc.sync.dma_start(dst, ot[:])
 
-        first_product(0)
-        gates(0)
-        first_product(1)
-        seats(0)
-        gates(1)
-        seats(1)
-        put(0)
-        put(1)
+        for u in range(2):
+            for t in range(2):
+                first_product(t, slice(P * u, P * (u + 1)))
         for t in range(2, PACK):
-            first_product(t)
-            gates(t)
-            seats(t)
-            take(t - 2, 0)
-            put(t)
-        take(2, 0)
-        take(3, 0)
-        second_product(0)
-        hid.append(sb.tile([P, PACK * HALF], BF16, name="hid1", tag=f"h{PACK - 1}", align_bytes=64))
-        for t in range(PACK):
-            take(t, 1)
-        second_product(1)
+            first_product(t, slice(0, J))
+        empty(0)
+        empty(1)
+        h1.extend([sb.tile([P, I], F32, name=f"h{t}", tag=f"h{t}", align_bytes=64) for t in range(PACK)])
+        look_up(0)
+        look_up(1)
+        gates(0)
+        gates(1)
+        look_up(2)
+        seats(0)
+        put(0)
+        seats(1)
+        put(1)
+        a_t.append(sb.tile([P, J], F32, name="a2", tag="a0", align_bytes=64))
+        empty(2)
+        g1.append(sb.tile([P, I], F32, name="g2", tag="g0", align_bytes=64))
+        gates(2)
+        cg.append(sb.tile([P, I], U8, name="cg3", tag="g1", align_bytes=64))
+        look_up(3)
+        seats(2)
+        put(2)
+        g1.append(sb.tile([P, I], F32, name="g3", tag="g3", align_bytes=64))
+        gates(3)
+        a_t.append(sb.tile([P, J], F32, name="a3", tag="a1", align_bytes=64))
+        empty(3)
+        seats(3)
+        put(3)
+        hid.append(sb.tile([P, PACK * HALF], BF16, name="hid0", tag="g3", align_bytes=64))
+        hid.append(sb.tile([P, PACK * HALF], BF16, name="hid1", tag="a1", align_bytes=64))
+        for u in range(2):
+            for t in range(PACK):
+                take(t, u)
+            second_product(u)

@@ -68,13 +68,11 @@ def tile_list_relayed_kernel(tc, xt_words, xt_scales, w_words, w_scales, ca, st,
         nc.scalar.dma_start(ww[:].bitcast(I32), w_words[0].bitcast(I32))
         nc.sync.dma_start(l3[:], offs3)
         nc.scalar.dma_start(st_t[:], st.rearrange("(p t) o -> p (t o)", t=PACK))
-        nc.sync.dma_start(cat[0][:], ca_rows[0])
+        for t in range(PACK):
+            nc.sync.dma_start(cat[t][:], ca_rows[t])
         nc.sync.dma_start(l2[:], offs2)
-        nc.sync.dma_start(cat[1][:], ca_rows[1])
-        nc.sync.dma_start(cat[2][:], ca_rows[2])
         nc.sync.dma_start(sa_t[:], sa.rearrange("(p t) o -> p (t o)", t=PACK))
         nc.sync.dma_start(l4[:], offs4)
-        nc.sync.dma_start(cat[3][:], ca_rows[3])
         nc.sync.dma_start(l5[:], offs5)
         nc.sync.dma_start(wbw[:].bitcast(I32), wb_words[0].bitcast(I32))
         for q in range(4):
@@ -85,7 +83,7 @@ def tile_list_relayed_kernel(tc, xt_words, xt_scales, w_words, w_scales, ca, st,
         nc.vector.tensor_copy(xsg[:], xs[:].indirect(l1[:]))
         wsd = sb.tile([P, PACK, P], U8, name="wsd", align_bytes=64)
         wwd0 = sb.tile([P, P], U16, name="wwd0", align_bytes=64)
-        wwd1 = sb.tile([P, P], U16, name="wwd1", align_bytes=64)
+        wwd1 = sb.tile([P, P], U16, name="wwd1", tag="wwd1", align_bytes=64)
         wwdr = sb.tile([P, PACK - 2, P], U16, name="wwdr", align_bytes=64)
         wwd = [wwd0[:], wwd1[:]] + [wwdr[:, t, :] for t in range(PACK - 2)]
         ww_by_t = ww[:].bitcast(U16).rearrange("p (m t) -> p t m", t=PACK)
@@ -97,13 +95,10 @@ def tile_list_relayed_kernel(tc, xt_words, xt_scales, w_words, w_scales, ca, st,
         nc.scalar.copy(wwd1[:], ww_by_t[:, 1, :])
         nc.scalar.copy(wwdr[:], ww_by_t[:, 2:, :])
 
-        acc01 = ps.tile([P, 2, J], F32, name="acc01")
-        acc2 = ps.tile([P, J], F32, name="acc2")
-        acc3 = ps.tile([P, J], F32, name="acc3")
-        acc = [acc01[:, 0, :], acc01[:, 1, :], acc2[:], acc3[:]]
+        acc = [ps.tile([P, J], F32, name=f"acc{t}") for t in range(PACK)]
         a_t = [sb.tile([P, J], F32, name=f"a{t}", tag=f"a{t}", align_bytes=64) for t in range(2)]
-        cg = [sb.tile([P, I], U8, name=f"cg{t}", align_bytes=64) for t in range(PACK - 1)]
-        g1 = [sb.tile([P, I], F32, name=f"g{t}", tag=f"g{t}", align_bytes=64) for t in range(2)]
+        cg = [sb.tile([P, I], U8, name=f"cg{t}", align_bytes=64) for t in range(PACK)]
+        g1 = [sb.tile([P, I], F32, name="g0", align_bytes=64)]
         hid = []
         h1 = []
 
@@ -115,13 +110,13 @@ def tile_list_relayed_kernel(tc, xt_words, xt_scales, w_words, w_scales, ca, st,
             nc.vector.tensor_copy(cg[t][:], cat[t][:].indirect(l3[:]))
 
         def gates(t):
-            nc.vector.tensor_scalar(g1[t][:], cg[t][:].bitcast(E4M3), st_t[:, t : t + 1], None, MULT)
+            nc.scalar.activation(g1[t][:], cg[t][:].bitcast(E4M3), COPY, scale=st_t[:, t : t + 1])
 
         def empty(t):
             if t < 2:
-                nc.scalar.copy(a_t[t][:], acc[t])
+                nc.scalar.copy(a_t[t][:], acc[t][:])
             else:
-                nc.vector.tensor_copy(a_t[t][:], acc[t])
+                nc.vector.tensor_copy(a_t[t][:], acc[t][:])
 
         def seats(t):
             nc.vector.tensor_tensor(h1[t][:], a_t[t][:].indirect(l2[:]), g1[t][:], MULT)
@@ -135,7 +130,7 @@ def tile_list_relayed_kernel(tc, xt_words, xt_scales, w_words, w_scales, ca, st,
                                  pw[t][:].indirect(l5[:, u * cols : (u + 1) * cols]), COPY)
 
         def second_product(u):
-            hq = sb.tile([P, HALF], U32, name=f"hq{u}", align_bytes=64)
+            hq = sb.tile([P, HALF], U32, name=f"hq{u}", tag="hq", align_bytes=64)
             hs = sb.tile([P, HALF], U8, name=f"hs{u}", align_bytes=64)
             nc.vector.quantize_mx(out=hq[:].bitcast(E4M3X4), scales=hs[:], in_=hid[u][:])
             for h in range(2):
@@ -153,37 +148,29 @@ def tile_list_relayed_kernel(tc, xt_words, xt_scales, w_words, w_scales, ca, st,
                     nc.sync.dma_start(dst, ot[:])
 
         for u in range(2):
-            for t in range(2):
-                first_product(t, slice(P * u, P * (u + 1)))
-        for t in range(2, PACK):
+            first_product(0, slice(P * u, P * (u + 1)))
+        for t in range(1, PACK):
             first_product(t, slice(0, J))
+        for t in range(PACK):
+            look_up(t)
+        gates(0)
         empty(0)
         empty(1)
+        g_late = sb.tile([P, PACK - 1, I], F32, name="g_late", tag="wwd1", align_bytes=64)
+        g1.extend([g_late[:, t, :] for t in range(PACK - 1)])
+        for t in range(1, PACK):
+            gates(t)
         h1.extend([sb.tile([P, I], F32, name=f"h{t}", tag=f"h{t}", align_bytes=64) for t in range(PACK)])
-        look_up(0)
-        look_up(1)
-        gates(0)
-        gates(1)
-        look_up(2)
-        seats(0)
-        put(0)
-        seats(1)
-        put(1)
+        for t in range(2):
+            seats(t)
+            put(t)
         a_t.append(sb.tile([P, J], F32, name="a2", tag="a0", align_bytes=64))
-        empty(2)
-        g1.append(sb.tile([P, I], F32, name="g2", tag="g0", align_bytes=64))
-        gates(2)
-        cg.append(sb.tile([P, I], U8, name="cg3", tag="g1", align_bytes=64))
-        look_up(3)
-        seats(2)
-        put(2)
-        g1.append(sb.tile([P, I], F32, name="g3", tag="g3", align_bytes=64))
-        gates(3)
         a_t.append(sb.tile([P, J], F32, name="a3", tag="a1", align_bytes=64))
-        empty(3)
-        seats(3)
-        put(3)
-        hid.append(sb.tile([P, PACK * HALF], BF16, name="hid0", tag="g3", align_bytes=64))
+        for t in range(2, PACK):
+            empty(t)
+            seats(t)
+            put(t)
+        hid.append(sb.tile([P, PACK * HALF], BF16, name="hid0", tag="wwd1", align_bytes=64))
         hid.append(sb.tile([P, PACK * HALF], BF16, name="hid1", tag="a1", align_bytes=64))
         for u in range(2):
             for t in range(PACK):

@@ -51,9 +51,9 @@ def tile_list_relayed_kernel(tc, xt_words, xt_scales, w_words, w_scales, ca, st,
 
         nc.vector.memset(xs[:].bitcast(I32), 0)
         nc.vector.memset(wsraw[:].bitcast(I32), 0)
-        nc.gpsimd.memset(wbs[:].bitcast(I32), 0)
+        nc.vector.memset(wbs[:].bitcast(I32), 0)
         for t in range(PACK):
-            (nc.vector if t < 2 else nc.gpsimd).memset(pw[t][:], 0.0)
+            nc.vector.memset(pw[t][:], 0.0)
 
         ca_rows = ca.rearrange("(p t) v -> t p v", t=PACK)
         def load_xs(queue, q):
@@ -65,9 +65,9 @@ def tile_list_relayed_kernel(tc, xt_words, xt_scales, w_words, w_scales, ca, st,
         for q in range(4):
             load_xs(nc.sync if q % 2 == 0 else nc.scalar, q)
         nc.sync.dma_start(xw[:], xt_words[0].rearrange("p c r -> p (c r)").bitcast(I32))
-        nc.scalar.dma_start(ww[:].bitcast(I32), w_words[0].bitcast(I32))
+        nc.sync.dma_start(ww[:].bitcast(I32), w_words[0].bitcast(I32))
         nc.sync.dma_start(l3[:], offs3)
-        nc.scalar.dma_start(st_t[:], st.rearrange("(p t) o -> p (t o)", t=PACK))
+        nc.sync.dma_start(st_t[:], st.rearrange("(p t) o -> p (t o)", t=PACK))
         for t in range(PACK):
             nc.sync.dma_start(cat[t][:], ca_rows[t])
         nc.sync.dma_start(l2[:], offs2)

from contextlib import ExitStack

import concourse.mybir as mybir

K, T, J, R, C, V, I, O, N = 512, 1024, 256, 512, 512, 512, 128, 256, 256
FLOPS = 2 * K * R * J + 2 * R * N * O

F32 = mybir.dt.float32
BF16 = mybir.dt.bfloat16
I32 = mybir.dt.int32
U32 = mybir.dt.uint32
U16 = mybir.dt.uint16
U8 = mybir.dt.uint8
E4M3 = mybir.dt.float8_e4m3fn
E4M3X4 = mybir.dt.float8_e4m3fn_x4
E5M2X4 = mybir.dt.float8_e5m2_x4
E2M1X4 = mybir.dt.float4_e2m1fn_x4
COPY = mybir.ActivationFunctionType.Copy
MULT = mybir.AluOpType.mult

P = 128
PACK = 4
HALF = O // 2


def tile_list_relayed_kernel(tc, xt_words, xt_scales, w_words, w_scales, ca, st, sa, wb_words, wb_scales,
                                offs, offs2, offs3, offs4, offs5, out):
    nc = tc.nc
    with ExitStack() as ctx:
        sb = ctx.enter_context(tc.tile_pool(name="sb", bufs=1))
        ps = ctx.enter_context(tc.psum_pool(name="ps", bufs=1))

        l1 = sb.tile([P, J // 16], U16, name="l1")
        l2 = sb.tile([P, I // 16], U16, name="l2")
        l3 = sb.tile([P, I // 16], U16, name="l3")
        l4 = sb.tile([P, I // 16], U16, name="l4")
        l5 = sb.tile([P, O // 16], U16, name="l5")

        xw = sb.tile([P, T], I32, name="xw", align_bytes=64)
        xs = sb.tile([P, T], U8, name="xs", tag="xs", align_bytes=64)
        xsg = sb.tile([P, J], U8, name="xsg", align_bytes=64)
        ww = sb.tile([P, 2 * R], U8, name="ww", align_bytes=64)
        wstage = sb.tile([PACK, R], I32, name="wstage", align_bytes=64)
        wsraw = sb.tile([P, R], U8, name="wsraw", align_bytes=64)
        wbw = sb.tile([P, 2 * N], U8, name="wbw", align_bytes=64)
        wbs = sb.tile([P, N], U8, name="wbs", align_bytes=64)
        st_t = sb.tile([P, PACK], F32, name="st_t")
        sa_t = sb.tile([P, PACK], F32, name="sa_t")
        cat = [sb.tile([P, V], U8, name=f"cat{t}", align_bytes=64) for t in range(PACK)]
        pw = [sb.tile([P, C], F32, name=f"pw{t}", align_bytes=64) for t in range(PACK)]

        nc.vector.memset(xs[:].bitcast(I32), 0)
        nc.vector.memset(wsraw[:].bitcast(I32), 0)
        nc.vector.memset(wbs[:].bitcast(I32), 0)
        for t in range(PACK):
            nc.vector.memset(pw[t][:], 0.0)

        ca_rows = ca.rearrange("(p t) v -> t p v", t=PACK)
        def load_xs(queue, q):
            queue.dma_start(xs[32 * q : 32 * q + 4, :].bitcast(I32), xt_scales[0, 4 * q : 4 * q + 4, :].bitcast(I32))

        nc.sync.dma_start(l1[:], offs)
        nc.scalar.dma_start(wstage[:].rearrange("r (q c) -> r q c", q=4),
                            w_scales[0].bitcast(I32).rearrange("(q r) c -> r q c", r=4))
        for q in range(4):
            load_xs(nc.sync if q % 2 == 0 else nc.scalar, q)
        nc.sync.dma_start(xw[:], xt_words[0].rearrange("p c r -> p (c r)").bitcast(I32))
        nc.sync.dma_start(ww[:].bitcast(I32), w_words[0].bitcast(I32))
        nc.sync.dma_start(l3[:], offs3)
        nc.sync.dma_start(st_t[:], st.rearrange("(p t) o -> p (t o)", t=PACK))
        for t in range(PACK):
            nc.sync.dma_start(cat[t][:], ca_rows[t])
        nc.sync.dma_start(l2[:], offs2)
        nc.sync.dma_start(sa_t[:], sa.rearrange("(p t) o -> p (t o)", t=PACK))
        nc.sync.dma_start(l4[:], offs4)
        nc.sync.dma_start(l5[:], offs5)
        nc.sync.dma_start(wbw[:].bitcast(I32), wb_words[0].bitcast(I32))
        for q in range(4):
            nc.sync.dma_start(wbs[32 * q : 32 * q + 4, :].bitcast(I32), wb_scales[0, 4 * q : 4 * q + 4, :].bitcast(I32))

        for q in range(4):
            nc.vector.tensor_copy(wsraw[32 * q : 32 * q + 4, :].bitcast(I32), wstage[:, q * (R // 4) : (q + 1) * (R // 4)])
        nc.vector.tensor_copy(xsg[:], xs[:].indirect(l1[:]))
        wsd = sb.tile([P, PACK, P], U8, name="wsd", align_bytes=64)
        wwd0 = sb.tile([P, P], U16, name="wwd0", align_bytes=64)
        wwd1 = sb.tile([P, P], U16, name="wwd1", tag="wwd1", align_bytes=64)
        wwdr = sb.tile([P, PACK - 2, P], U16, name="wwdr", align_bytes=64)
        wwd = [wwd0[:], wwd1[:]] + [wwdr[:, t, :] for t in range(PACK - 2)]
        ww_by_t = ww[:].bitcast(U16).rearrange("p (m t) -> p t m", t=PACK)
        nc.vector.tensor_copy(wsd[:], wsraw[:].rearrange("p (m t) -> p t m", t=PACK))
        xwg = sb.tile([P, J], U32, name="xwg", align_bytes=64)
        for u in range(2):
            nc.vector.tensor_copy(xwg[:, P * u : P * (u + 1)], xw[:].bitcast(U32).indirect(l1[:, 8 * u : 8 * (u + 1)]))
        nc.scalar.copy(wwd0[:], ww_by_t[:, 0, :])
        nc.scalar.copy(wwd1[:], ww_by_t[:, 1, :])
        nc.scalar.copy(wwdr[:], ww_by_t[:, 2:, :])

        acc = [ps.tile([P, J], F32, name=f"acc{t}") for t in range(PACK)]
        a_t = [sb.tile([P, J], F32, name=f"a{t}", tag=f"a{t}", align_bytes=64) for t in range(2)]
        cg = [sb.tile([P, I], U8, name=f"cg{t}", align_bytes=64) for t in range(PACK)]
        g1 = [sb.tile([P, I], F32, name="g0", align_bytes=64)]
        hid = []
        h1 = []

        def first_product(t, cols):
            nc.tensor.matmul_mx(out=acc[t][:, cols], lhsT=wwd[t].bitcast(E2M1X4), lhsT_scale=wsd[:, t, :],
                                rhs=xwg[:, cols].bitcast(E5M2X4), rhs_scale=xsg[:, cols], start=True, stop=True)

        def look_up(t):
            nc.vector.tensor_copy(cg[t][:], cat[t][:].indirect(l3[:]))

        def gates(t):
            nc.scalar.activation(g1[t][:], cg[t][:].bitcast(E4M3), COPY, scale=st_t[:, t : t + 1])

        def empty(t):
            if t < 2:
                nc.scalar.copy(a_t[t][:], acc[t][:])
            else:
                nc.vector.tensor_copy(a_t[t][:], acc[t][:])

        def seats(t):
            nc.vector.tensor_tensor(h1[t][:], a_t[t][:].indirect(l2[:]), g1[t][:], MULT)

        def put(t):
            nc.scalar.activation(pw[t][:].indirect(l4[:]), h1[t][:], COPY, scale=sa_t[:, t : t + 1])

        def take(t, u):
            cols = HALF // 16
            nc.scalar.activation(hid[u][:].rearrange("p (c r) -> p c r", r=PACK)[:, :, t],
                                 pw[t][:].indirect(l5[:, u * cols : (u + 1) * cols]), COPY)

        def second_product(u):
            hq = sb.tile([P, HALF], U32, name=f"hq{u}", tag="hq", align_bytes=64)
            hs = sb.tile([P, HALF], U8, name=f"hs{u}", align_bytes=64)
            nc.vector.quantize_mx(out=hq[:].bitcast(E4M3X4), scales=hs[:], in_=hid[u][:])
            for h in range(2):
                res = ps.tile([P, HALF], F32, name=f"res{u}{h}")
                nc.tensor.matmul_mx(out=res[:], lhsT=wbw[:, 2 * P * h : 2 * P * (h + 1)].bitcast(E2M1X4),
                                    lhsT_scale=wbs[:, P * h : P * (h + 1)],
                                    rhs=hq[:].bitcast(E4M3X4), rhs_scale=hs[:], start=True, stop=True)
                ot = sb.tile([P, HALF], F32, name=f"ot{u}{h}", align_bytes=64)
                dst = out[P * h : P * (h + 1), HALF * u : HALF * (u + 1)]
                if u == 1 and h == 1:
                    nc.scalar.copy(ot[:], res[:])
                    nc.scalar.dma_start(dst, ot[:])
                else:
                    nc.vector.tensor_copy(ot[:], res[:])
                    nc.sync.dma_start(dst, ot[:])

        for u in range(2):
            first_product(0, slice(P * u, P * (u + 1)))
        for t in range(1, PACK):
            first_product(t, slice(0, J))
        for t in range(PACK):
            look_up(t)
        gates(0)
        empty(0)
        empty(1)
        g_late = sb.tile([P, PACK - 1, I], F32, name="g_late", tag="wwd1", align_bytes=64)
        g1.extend([g_late[:, t, :] for t in range(PACK - 1)])
        for t in range(1, PACK):
            gates(t)
        h1.extend([sb.tile([P, I], F32, name=f"h{t}", tag=f"h{t}", align_bytes=64) for t in range(PACK)])
        for t in range(2):
            seats(t)
            put(t)
        a_t.append(sb.tile([P, J], F32, name="a2", tag="a0", align_bytes=64))
        a_t.append(sb.tile([P, J], F32, name="a3", tag="a1", align_bytes=64))
        for t in range(2, PACK):
            empty(t)
            seats(t)
            put(t)
        hid.append(sb.tile([P, PACK * HALF], BF16, name="hid0", tag="wwd1", align_bytes=64))
        hid.append(sb.tile([P, PACK * HALF], BF16, name="hid1", tag="a1", align_bytes=64))
        for u in range(2):
            for t in range(PACK):
                take(t, u)
            second_product(u)
